import numpy as np
import ml_dtypes


def mxq(x, axis, fmt="e4m3"):
    dtype, down = {"e4m3": (ml_dtypes.float8_e4m3fn, 7), "e5m2": (ml_dtypes.float8_e5m2, 14)}[fmt]
    v = np.moveaxis(np.asarray(x, np.float32).astype(ml_dtypes.bfloat16).astype(np.float64), axis, -1)
    blocks = v.reshape(v.shape[:-1] + (-1, 32))
    amax = np.abs(blocks).max(-1, keepdims=True)
    byte = np.maximum(np.where(amax > 0, np.frexp(amax)[1] - 1 + 127, 0) - down, 1)
    scale = np.exp2(byte - 127.0)
    codes = (blocks / scale).astype(np.float32).astype(dtype).astype(np.float64)
    return np.moveaxis((codes * scale).reshape(v.shape), -1, axis)


WIDE = False


def mx_kscale(k):
    if not WIDE:
        return np.ones(k)
    levels = np.array([30, -30])
    if k % 512:
        return np.exp2(np.random.permutation(np.resize(levels, k // 32))).repeat(32)
    a = np.empty((k // 512, 16))
    for p in range(k // 512):
        a[p, :8] = np.random.permutation(np.resize(levels, 8))
        for g in range(8):
            far = levels[np.abs(levels - a[p, g]) >= 10]
            a[p, g + 8] = far[np.random.randint(len(far))]
    return np.exp2(a.ravel()).repeat(32)


def f64(x):
    return np.asarray(x).astype(np.float64)


def striped(idx):
    return np.tile(np.asarray(idx).reshape(-1, 16).T, (8, 1)).astype(np.uint16)


def unstriped(offs):
    return offs[:16].T.reshape(-1).astype(np.int64)


E2M1 = np.array([0.0, 0.5, 1.0, 1.5, 2.0, 3.0, 4.0, 6.0, -0.0, -0.5, -1.0, -1.5, -2.0, -3.0, -4.0, -6.0])


def pack_weight(w, fmt):
    k, n = w.shape
    w = f64(np.asarray(w, np.float32).astype(ml_dtypes.bfloat16)).reshape(k // 32, 32, n)
    amax = np.abs(w).max(1)
    if fmt in ("e4m3", "e5m2"):
        byte = np.frexp(amax)[1] - 1 + 127 - (7 if fmt == "e4m3" else 14)
    else:
        mant, ex = np.frexp(amax / 6.0)
        byte = np.where(mant > 0.5, ex, ex - 1) + 127
    byte = np.clip(np.where(amax > 0, byte, 1), 1, 254)
    scaled = (w * np.exp2(127.0 - byte)[:, None, :]).reshape(k, n).astype(np.float32)
    by_word = np.ascontiguousarray(scaled.reshape(k // 512, 128, 4, n).transpose(0, 1, 3, 2))
    if fmt in ("e4m3", "e5m2"):
        words = by_word.astype(ml_dtypes.float8_e4m3fn if fmt == "e4m3" else ml_dtypes.float8_e5m2).view(np.uint8)
    else:
        c = by_word.astype(ml_dtypes.float4_e2m1fn).view(np.uint8) & 0xF
        words = (c[..., 0::2] | (c[..., 1::2] << 4)).reshape(k // 512, 128, 2 * n)
    return np.ascontiguousarray(words), np.ascontiguousarray(byte.astype(np.uint8).reshape(k // 512, 16, n))


def unpack_weight(words, scales, fmt):
    g, _, n = scales.shape
    words = np.ascontiguousarray(words).reshape(g, 128, n, -1)
    if fmt in ("e4m3", "e5m2"):
        vals = words.view(ml_dtypes.float8_e4m3fn if fmt == "e4m3" else ml_dtypes.float8_e5m2).astype(np.float64)
    else:
        nib = np.empty((g, 128, n, 4), np.uint8)
        nib[..., 0::2] = words & 0xF
        nib[..., 1::2] = words >> 4
        vals = E2M1[nib]
    vals = vals * np.repeat(np.exp2(scales.astype(np.float64) - 127.0), 8, axis=1)[..., None]
    return vals.transpose(0, 1, 3, 2).reshape(g * 512, n)


K, T, J, R, V, N = 1024, 1024, 384, 512, 512, 256


def setup_inputs():
    n = np.random.standard_normal
    idx = np.random.permutation(T)[:J]
    idx2 = np.random.permutation(V)[:J]
    fk = mx_kscale(K)
    fr = mx_kscale(R)
    wp = pack_weight(n((K, R)) * 1 / np.sqrt(K) * fk[:, None] * fr, "e2m1")
    wbp = pack_weight(n((R, N)) * 1 / np.sqrt(R) / fr[:, None], "e5m2")
    return {
        "xf": (n((K, T))).astype(np.float32),
        "fk": (np.random.uniform(0.5, 2.0, (K, 1)) / fk[:, None]).astype(np.float32),
        "w_words": wp[0],
        "w_scales": wp[1],
        "tb": (n((R, V)) * 0.7).astype(np.float32),
        "wb_words": wbp[0],
        "wb_scales": wbp[1],
        "rs": (1.0 * n((J, N))).astype(np.float32),
        "offs": striped(idx),
        "offs2": striped(idx2),
    }


def reference(xf, fk, w_words, w_scales, tb, wb_words, wb_scales, rs, offs, offs2):
    idx = unstriped(offs)
    idx2 = unstriped(offs2)
    wu = unpack_weight(w_words, w_scales, "e2m1")
    wbu = unpack_weight(wb_words, wb_scales, "e5m2")
    xg = f64(xf)[:, idx]
    x1 = np.pad(xg, ((0, 0), (1, 0)))[:, :J]
    u = (xg - 0.6 * x1) * f64(fk)
    uq = mxq(u, 0, "e4m3")
    a = wu.T @ uq
    hid = np.maximum(a, 0.0) * f64(tb)[:, idx2]
    hidq = mxq(hid, 0, "e4m3")
    p = hidq.T @ wbu
    pk2 = np.max(np.abs(p), axis=1, keepdims=True)
    y = p / (pk2 + 0.2) + 0.3 * f64(rs)
    return y

@@ -1,0 +1,195 @@
+from contextlib import ExitStack
+
+import concourse.mybir as mybir
+
+K, T, J, R, V, N = 1024, 1024, 384, 512, 512, 256
+FLOPS = 2 * K * R * J + 2 * R * J * N
+
+F32 = mybir.dt.float32
+BF16 = mybir.dt.bfloat16
+I32 = mybir.dt.int32
+U32 = mybir.dt.uint32
+U16 = mybir.dt.uint16
+U8 = mybir.dt.uint8
+E4M3 = mybir.dt.float8_e4m3fn_x4
+E5M2 = mybir.dt.float8_e5m2_x4
+E2M1 = mybir.dt.float4_e2m1fn_x4
+ALU = mybir.AluOpType
+ACT = mybir.ActivationFunctionType
+
+P = 128
+PACK = 4
+PASSES = K // (P * PACK)
+CHUNK = 128
+CHUNKS = J // CHUNK
+PAD = 8
+
+
+def tile_list_steps_timestable_rowpeaks_kernel(tc, xf, fk, w_words, w_scales, tb, wb_words, wb_scales, rs, offs, offs2, out):
+    nc = tc.nc
+    with ExitStack() as ctx:
+        sb = ctx.enter_context(tc.tile_pool(name="sb", bufs=1))
+        ps = ctx.enter_context(tc.psum_pool(name="ps", bufs=1))
+
+        def cols(c):
+            return slice(c * CHUNK, (c + 1) * CHUNK)
+
+        def entries(c):
+            return slice(c * CHUNK // 16, (c + 1) * CHUNK // 16)
+
+        w_scale_raw = sb.tile([P, PASSES, R], U8, name="w_scale_raw", align_bytes=64)
+        wb_scale = sb.tile([P, N], U8, name="wb_scale", align_bytes=64)
+        nc.gpsimd.memset(w_scale_raw[:].bitcast(I32), 0)
+        nc.gpsimd.memset(wb_scale[:].bitcast(I32), 0)
+        scaled = [sb.tile([P, 2, PAD + J], F32, name=f"scaled{h}") for h in range(2 * PASSES)]
+        for h in range(2 * PASSES):
+            nc.vector.memset(scaled[h][:, :, PAD - 1 : PAD], 0.0)
+
+        x_list = sb.tile([P, J // 16], U16, name="x_list")
+        nc.sync.dma_start(x_list[:], offs)
+        factor = sb.tile([P, PASSES, PACK], F32, name="factor")
+        nc.sync.dma_start(factor[:], fk.rearrange("(a p t) o -> p a (t o)", a=PASSES, t=PACK))
+        w_raw = sb.tile([P, PASSES, R], U16, name="w_raw", align_bytes=64)
+        nc.sync.dma_start(w_raw[:].bitcast(I32), w_words.rearrange("a p b -> p a b").bitcast(I32))
+        x_rows = xf.rearrange("(a p t) n -> a t p n", a=PASSES, t=PACK)
+        x_plane = [sb.tile([P, T], F32, name=f"x_plane{i}") for i in range(PASSES * PACK)]
+        for i in range(5):
+            nc.sync.dma_start(x_plane[i][:], x_rows[i // PACK, i % PACK])
+        for q in range(4):
+            nc.sync.dma_start(
+                w_scale_raw[32 * q : 32 * q + 4, :, :].bitcast(I32),
+                w_scales[:, 4 * q : 4 * q + 4, :].rearrange("a r c -> r a c").bitcast(I32),
+            )
+        for i in range(5, PASSES * PACK):
+            nc.sync.dma_start(x_plane[i][:], x_rows[i // PACK, i % PACK])
+        tb_list = sb.tile([P, J // 16], U16, name="tb_list")
+        nc.sync.dma_start(tb_list[:], offs2)
+        tb_rows = tb.rearrange("(p t) v -> t p v", t=PACK)
+        tb_plane = [sb.tile([P, V], F32, name=f"tb_plane{t}") for t in range(PACK)]
+        for t in range(PACK):
+            nc.sync.dma_start(tb_plane[t][:], tb_rows[t])
+        wb_code = sb.tile([P, N], U32, name="wb_code", align_bytes=64)
+        nc.sync.dma_start(wb_code[:].bitcast(I32), wb_words[0].rearrange("p n t -> p (n t)").bitcast(I32))
+        for q in range(4):
+            nc.sync.dma_start(
+                wb_scale[32 * q : 32 * q + 4, :].bitcast(I32),
+                wb_scales[0, 4 * q : 4 * q + 4, :].bitcast(I32),
+            )
+        resid = sb.tile([P, CHUNKS, N], F32, name="resid")
+        nc.sync.dma_start(resid[:], rs.rearrange("(c p) n -> p c n", p=P))
+
+        w_code = sb.tile([P, PASSES, PACK, P], U16, name="w_code", align_bytes=64)
+        nc.vector.tensor_copy(w_code[:], w_raw[:].rearrange("p a (q t) -> p a t q", t=PACK))
+        w_scale = sb.tile([P, PASSES, PACK, P], U8, name="w_scale", align_bytes=64)
+        nc.vector.tensor_copy(w_scale[:], w_scale_raw[:].rearrange("p a (q t) -> p a t q", t=PACK))
+
+        picked = [sb.tile([P, J], F32, name=f"picked{i}") for i in range(PASSES * PACK)]
+        pairs = [sb.tile([P, 2, J, 2], BF16, name=f"pairs{a}") for a in range(PASSES)]
+        u = [sb.tile([P, J, PACK], BF16, name=f"u{a}", align_bytes=64) for a in range(PASSES)]
+        u_code = [sb.tile([P, J], U32, name=f"u_code{a}", align_bytes=64) for a in range(PASSES)]
+        u_scale = [sb.tile([P, J], U8, name=f"u_scale{a}", align_bytes=64) for a in range(PASSES)]
+        first = [ps.tile([P, PACK, CHUNK], F32, name=f"first{c}") for c in range(CHUNKS)]
+
+        def pick(i, lo, hi):
+            nc.scalar.activation(picked[i][:, lo:hi], x_plane[i][:].indirect(x_list[:, lo // 16 : hi // 16]), ACT.Copy)
+
+        def scale(i, lo, hi):
+            a, t = divmod(i, PACK)
+            nc.vector.tensor_scalar(
+                scaled[i // 2][:, i % 2, PAD + lo : PAD + hi], picked[i][:, lo:hi], factor[:, a, t : t + 1], None, ALU.mult
+            )
+
+        def steps(h, lo, hi):
+            nc.vector.scalar_tensor_tensor(
+                pairs[h // 2][:, h % 2, lo:hi, :],
+                scaled[h][:, :, PAD - 1 + lo : PAD - 1 + hi].rearrange("p e j -> p j e"),
+                -0.6,
+                scaled[h][:, :, PAD + lo : PAD + hi].rearrange("p e j -> p j e"),
+                ALU.mult,
+                ALU.add,
+            )
+
+        def weave(a, lo, hi):
+            words = pairs[a][:].rearrange("p h j e -> p h (j e)").bitcast(I32)
+            nc.vector.tensor_copy(u[a][:, lo:hi, :].bitcast(I32), words[:, :, lo:hi].rearrange("p h j -> p j h"))
+
+        def quantise_u(a, lo, hi):
+            nc.vector.quantize_mx(
+                out=u_code[a][:, lo:hi].bitcast(E4M3),
+                scales=u_scale[a][:, lo:hi],
+                in_=u[a][:, lo:hi, :].rearrange("p j t -> p (j t)"),
+            )
+
+        def first_product(a, c):
+            for t in range(PACK):
+                nc.tensor.matmul_mx(
+                    out=first[c][:, t, :],
+                    lhsT=w_code[:, a, t, :].bitcast(E2M1),
+                    lhsT_scale=w_scale[:, a, t, :],
+                    rhs=u_code[a][:, cols(c)].bitcast(E4M3),
+                    rhs_scale=u_scale[a][:, cols(c)],
+                    start=(a == 0 and t == 0),
+                    stop=(a == PASSES - 1 and t == PACK - 1),
+                )
+
+        last = PASSES * PACK - 1
+        for i in range(last):
+            pick(i, 0, J)
+            scale(i, 0, J)
+            if i % 2 == 1:
+                steps(i // 2, 0, J)
+            if i == PACK - 1:
+                weave(0, 0, J)
+                quantise_u(0, 0, J)
+                for c in range(CHUNKS):
+                    first_product(0, c)
+        for c in range(CHUNKS):
+            lo, hi = c * CHUNK, (c + 1) * CHUNK
+            pick(last, lo, hi)
+            scale(last, lo, hi)
+            steps(last // 2, lo, hi)
+            weave(1, lo, hi)
+            quantise_u(1, lo, hi)
+            first_product(1, c)
+
+        tb_picked = [sb.tile([P, PACK, CHUNK], F32, name=f"tb_picked{c}") for c in range(CHUNKS)]
+        for c in range(CHUNKS):
+            for t in range(PACK):
+                nc.scalar.activation(tb_picked[c][:, t, :], tb_plane[t][:].indirect(tb_list[:, entries(c)]), ACT.Copy)
+
+        resid_part = sb.tile([P, CHUNKS, N], F32, name="resid_part")
+        for c in range(CHUNKS):
+            hid = sb.tile([P, CHUNK, PACK], BF16, name=f"hid{c}", align_bytes=64)
+            nc.vector.scalar_tensor_tensor(
+                hid[:],
+                first[c][:].rearrange("p t j -> p j t"),
+                0.0,
+                tb_picked[c][:].rearrange("p t j -> p j t"),
+                ALU.max,
+                ALU.mult,
+            )
+            hid_code = sb.tile([P, CHUNK], U32, name=f"hid_code{c}", align_bytes=64)
+            hid_scale = sb.tile([P, CHUNK], U8, name=f"hid_scale{c}", align_bytes=64)
+            nc.vector.quantize_mx(
+                out=hid_code[:].bitcast(E4M3), scales=hid_scale[:], in_=hid[:].rearrange("p j t -> p (j t)")
+            )
+            second = ps.tile([P, N], F32, name=f"second{c}")
+            nc.tensor.matmul_mx(
+                out=second[:],
+                lhsT=hid_code[:].bitcast(E4M3),
+                lhsT_scale=hid_scale[:],
+                rhs=wb_code[:].bitcast(E5M2),
+                rhs_scale=wb_scale[:],
+                start=True,
+                stop=True,
+            )
+            nc.scalar.activation(resid_part[:, c, :], resid[:, c, :], ACT.Copy, scale=0.3)
+            size = sb.tile([P, N], F32, name=f"size{c}")
+            nc.scalar.activation(size[:], second[:], ACT.Abs)
+            divisor = sb.tile([P, 1], F32, name=f"divisor{c}")
+            nc.vector.tensor_scalar(size[:], size[:], 0.2, None, ALU.add, ALU.max, accum_out=divisor[:])
+            inverse = sb.tile([P, 1], F32, name=f"inverse{c}")
+            nc.vector.reciprocal(inverse[:], divisor[:])
+            result = sb.tile([P, N], F32, name=f"result{c}")
+            nc.vector.scalar_tensor_tensor(result[:], second[:], inverse[:], resid_part[:, c, :], ALU.mult, ALU.add)
+            nc.sync.dma_start(out[cols(c), :], result[:])

@@ -42,32 +42,38 @@ def tile_list_steps_timestable_rowpeaks_kernel(tc, xf, fk, w_words, w_scales, tb
         nc.gpsimd.memset(w_scale_raw[:].bitcast(I32), 0)
         nc.gpsimd.memset(wb_scale[:].bitcast(I32), 0)
         scaled = [sb.tile([P, 2, PAD + J], F32, name=f"scaled{h}") for h in range(2 * PASSES)]
+        zero = sb.tile([P, 2, 1], F32, name="zero")
+        nc.vector.memset(zero[:], 0.0)
         for h in range(2 * PASSES):
-            nc.vector.memset(scaled[h][:, :, PAD - 1 : PAD], 0.0)
+            nc.scalar.activation(scaled[h][:, :, PAD - 1 : PAD], zero[:], ACT.Copy)
 
         x_list = sb.tile([P, J // 16], U16, name="x_list")
         nc.sync.dma_start(x_list[:], offs)
         factor = sb.tile([P, PASSES, PACK], F32, name="factor")
         nc.sync.dma_start(factor[:], fk.rearrange("(a p t) o -> p a (t o)", a=PASSES, t=PACK))
         w_raw = sb.tile([P, PASSES, R], U16, name="w_raw", align_bytes=64)
-        nc.sync.dma_start(w_raw[:].bitcast(I32), w_words.rearrange("a p b -> p a b").bitcast(I32))
         x_rows = xf.rearrange("(a p t) n -> a t p n", a=PASSES, t=PACK)
         x_plane = [sb.tile([P, T], F32, name=f"x_plane{i}") for i in range(PASSES * PACK)]
-        for i in range(5):
-            nc.sync.dma_start(x_plane[i][:], x_rows[i // PACK, i % PACK])
+        nc.sync.dma_start(x_plane[0][:], x_rows[0, 0])
         for q in range(4):
             nc.sync.dma_start(
                 w_scale_raw[32 * q : 32 * q + 4, :, :].bitcast(I32),
                 w_scales[:, 4 * q : 4 * q + 4, :].rearrange("a r c -> r a c").bitcast(I32),
             )
-        for i in range(5, PASSES * PACK):
-            nc.sync.dma_start(x_plane[i][:], x_rows[i // PACK, i % PACK])
+        nc.sync.dma_start(w_raw[:].bitcast(I32), w_words.rearrange("a p b -> p a b").bitcast(I32))
         tb_list = sb.tile([P, J // 16], U16, name="tb_list")
-        nc.sync.dma_start(tb_list[:], offs2)
-        tb_rows = tb.rearrange("(p t) v -> t p v", t=PACK)
-        tb_plane = [sb.tile([P, V], F32, name=f"tb_plane{t}") for t in range(PACK)]
-        for t in range(PACK):
-            nc.sync.dma_start(tb_plane[t][:], tb_rows[t])
+        tb_rows = tb.rearrange("(p t) v -> p t v", t=PACK)
+        tb_first = sb.tile([P, V], F32, name="tb_first")
+        tb_second = sb.tile([P, V], F32, name="tb_second")
+        tb_rest = sb.tile([P, 2, V], F32, name="tb_rest")
+        tb_plane = [tb_first[:], tb_second[:], tb_rest[:, 0, :], tb_rest[:, 1, :]]
+        for i in range(1, PASSES * PACK):
+            nc.sync.dma_start(x_plane[i][:], x_rows[i // PACK, i % PACK])
+            if i == PACK - 1:
+                nc.sync.dma_start(tb_list[:], offs2)
+                nc.sync.dma_start(tb_first[:], tb_rows[:, 0, :])
+        nc.sync.dma_start(tb_second[:], tb_rows[:, 1, :])
+        nc.sync.dma_start(tb_rest[:], tb_rows[:, 2:4, :])
         wb_code = sb.tile([P, N], U32, name="wb_code", align_bytes=64)
         nc.sync.dma_start(wb_code[:].bitcast(I32), wb_words[0].rearrange("p n t -> p (n t)").bitcast(I32))
         for q in range(4):
@@ -155,7 +161,7 @@ def tile_list_steps_timestable_rowpeaks_kernel(tc, xf, fk, w_words, w_scales, tb
         tb_picked = [sb.tile([P, PACK, CHUNK], F32, name=f"tb_picked{c}") for c in range(CHUNKS)]
         for c in range(CHUNKS):
             for t in range(PACK):
-                nc.scalar.activation(tb_picked[c][:, t, :], tb_plane[t][:].indirect(tb_list[:, entries(c)]), ACT.Copy)
+                nc.scalar.activation(tb_picked[c][:, t, :], tb_plane[t].indirect(tb_list[:, entries(c)]), ACT.Copy)
 
         resid_part = sb.tile([P, CHUNKS, N], F32, name="resid_part")
         for c in range(CHUNKS):
@@ -183,7 +189,7 @@ def tile_list_steps_timestable_rowpeaks_kernel(tc, xf, fk, w_words, w_scales, tb
                 start=True,
                 stop=True,
             )
-            nc.scalar.activation(resid_part[:, c, :], resid[:, c, :], ACT.Copy, scale=0.3)
+            nc.gpsimd.tensor_scalar(resid_part[:, c, :], resid[:, c, :], 0.3, 0.0, ALU.mult, ALU.add)
             size = sb.tile([P, N], F32, name=f"size{c}")
             nc.scalar.activation(size[:], second[:], ACT.Abs)
             divisor = sb.tile([P, 1], F32, name=f"divisor{c}")

@@ -50,7 +50,6 @@ def tile_list_steps_timestable_rowpeaks_kernel(tc, xf, fk, w_words, w_scales, tb
         x_list = sb.tile([P, J // 16], U16, name="x_list")
         nc.sync.dma_start(x_list[:], offs)
         factor = sb.tile([P, PASSES, PACK], F32, name="factor")
-        nc.sync.dma_start(factor[:], fk.rearrange("(a p t) o -> p a (t o)", a=PASSES, t=PACK))
         w_raw = sb.tile([P, PASSES, R], U16, name="w_raw", align_bytes=64)
         x_rows = xf.rearrange("(a p t) n -> a t p n", a=PASSES, t=PACK)
         x_plane = [sb.tile([P, T], F32, name=f"x_plane{i}") for i in range(PASSES * PACK)]
@@ -64,16 +63,16 @@ def tile_list_steps_timestable_rowpeaks_kernel(tc, xf, fk, w_words, w_scales, tb
         tb_list = sb.tile([P, J // 16], U16, name="tb_list")
         tb_rows = tb.rearrange("(p t) v -> p t v", t=PACK)
         tb_first = sb.tile([P, V], F32, name="tb_first")
-        tb_second = sb.tile([P, V], F32, name="tb_second")
-        tb_rest = sb.tile([P, 2, V], F32, name="tb_rest")
-        tb_plane = [tb_first[:], tb_second[:], tb_rest[:, 0, :], tb_rest[:, 1, :]]
+        tb_rest = sb.tile([P, PACK - 1, V], F32, name="tb_rest")
+        tb_plane = [tb_first[:]] + [tb_rest[:, t, :] for t in range(PACK - 1)]
         for i in range(1, PASSES * PACK):
             nc.sync.dma_start(x_plane[i][:], x_rows[i // PACK, i % PACK])
+            if i == 1:
+                nc.sync.dma_start(factor[:], fk.rearrange("(a p t) o -> p a (t o)", a=PASSES, t=PACK))
             if i == PACK - 1:
                 nc.sync.dma_start(tb_list[:], offs2)
-                nc.sync.dma_start(tb_first[:], tb_rows[:, 0, :])
-        nc.sync.dma_start(tb_second[:], tb_rows[:, 1, :])
-        nc.sync.dma_start(tb_rest[:], tb_rows[:, 2:4, :])
+        nc.sync.dma_start(tb_first[:], tb_rows[:, 0, :])
+        nc.sync.dma_start(tb_rest[:], tb_rows[:, 1:PACK, :])
         wb_code = sb.tile([P, N], U32, name="wb_code", align_bytes=64)
         nc.sync.dma_start(wb_code[:].bitcast(I32), wb_words[0].rearrange("p n t -> p (n t)").bitcast(I32))
         for q in range(4):
@@ -189,7 +188,7 @@ def tile_list_steps_timestable_rowpeaks_kernel(tc, xf, fk, w_words, w_scales, tb
                 start=True,
                 stop=True,
             )
-            nc.gpsimd.tensor_scalar(resid_part[:, c, :], resid[:, c, :], 0.3, 0.0, ALU.mult, ALU.add)
+            nc.scalar.activation(resid_part[:, c, :], resid[:, c, :], ACT.Copy, scale=0.3)
             size = sb.tile([P, N], F32, name=f"size{c}")
             nc.scalar.activation(size[:], second[:], ACT.Abs)
             divisor = sb.tile([P, 1], F32, name=f"divisor{c}")

from contextlib import ExitStack

import concourse.mybir as mybir

K, T, J, R, V, N = 1024, 1024, 384, 512, 512, 256
FLOPS = 2 * K * R * J + 2 * R * J * N

F32 = mybir.dt.float32
BF16 = mybir.dt.bfloat16
I32 = mybir.dt.int32
U32 = mybir.dt.uint32
U16 = mybir.dt.uint16
U8 = mybir.dt.uint8
E4M3 = mybir.dt.float8_e4m3fn_x4
E5M2 = mybir.dt.float8_e5m2_x4
E2M1 = mybir.dt.float4_e2m1fn_x4
ALU = mybir.AluOpType
ACT = mybir.ActivationFunctionType

P = 128
PACK = 4
PASSES = K // (P * PACK)
CHUNK = 128
CHUNKS = J // CHUNK
PAD = 8


def tile_list_steps_timestable_rowpeaks_kernel(tc, xf, fk, w_words, w_scales, tb, wb_words, wb_scales, rs, offs, offs2, out):
    nc = tc.nc
    with ExitStack() as ctx:
        sb = ctx.enter_context(tc.tile_pool(name="sb", bufs=1))
        ps = ctx.enter_context(tc.psum_pool(name="ps", bufs=1))

        def cols(c):
            return slice(c * CHUNK, (c + 1) * CHUNK)

        def entries(c):
            return slice(c * CHUNK // 16, (c + 1) * CHUNK // 16)

        w_scale_raw = sb.tile([P, PASSES, R], U8, name="w_scale_raw", align_bytes=64)
        wb_scale = sb.tile([P, N], U8, name="wb_scale", align_bytes=64)
        nc.gpsimd.memset(w_scale_raw[:].bitcast(I32), 0)
        nc.gpsimd.memset(wb_scale[:].bitcast(I32), 0)
        scaled = [sb.tile([P, 2, PAD + J], F32, name=f"scaled{h}") for h in range(2 * PASSES)]
        zero = sb.tile([P, 2, 1], F32, name="zero")
        nc.vector.memset(zero[:], 0.0)
        for h in range(2 * PASSES):
            nc.scalar.activation(scaled[h][:, :, PAD - 1 : PAD], zero[:], ACT.Copy)

        x_list = sb.tile([P, J // 16], U16, name="x_list")
        nc.sync.dma_start(x_list[:], offs)
        factor = sb.tile([P, PASSES, PACK], F32, name="factor")
        w_raw = sb.tile([P, PASSES, R], U16, name="w_raw", align_bytes=64)
        x_rows = xf.rearrange("(a p t) n -> a t p n", a=PASSES, t=PACK)
        x_plane = [sb.tile([P, T], F32, name=f"x_plane{i}") for i in range(PASSES * PACK)]
        nc.sync.dma_start(x_plane[0][:], x_rows[0, 0])
        for q in range(4):
            nc.sync.dma_start(
                w_scale_raw[32 * q : 32 * q + 4, :, :].bitcast(I32),
                w_scales[:, 4 * q : 4 * q + 4, :].rearrange("a r c -> r a c").bitcast(I32),
            )
        nc.sync.dma_start(w_raw[:].bitcast(I32), w_words.rearrange("a p b -> p a b").bitcast(I32))
        tb_list = sb.tile([P, J // 16], U16, name="tb_list")
        tb_rows = tb.rearrange("(p t) v -> p t v", t=PACK)
        tb_first = sb.tile([P, V], F32, name="tb_first")
        tb_rest = sb.tile([P, PACK - 1, V], F32, name="tb_rest")
        tb_plane = [tb_first[:]] + [tb_rest[:, t, :] for t in range(PACK - 1)]
        for i in range(1, PASSES * PACK):
            nc.sync.dma_start(x_plane[i][:], x_rows[i // PACK, i % PACK])
            if i == 1:
                nc.sync.dma_start(factor[:], fk.rearrange("(a p t) o -> p a (t o)", a=PASSES, t=PACK))
            if i == PACK - 1:
                nc.sync.dma_start(tb_list[:], offs2)
        nc.sync.dma_start(tb_first[:], tb_rows[:, 0, :])
        nc.sync.dma_start(tb_rest[:], tb_rows[:, 1:PACK, :])
        wb_code = sb.tile([P, N], U32, name="wb_code", align_bytes=64)
        nc.sync.dma_start(wb_code[:].bitcast(I32), wb_words[0].rearrange("p n t -> p (n t)").bitcast(I32))
        for q in range(4):
            nc.sync.dma_start(
                wb_scale[32 * q : 32 * q + 4, :].bitcast(I32),
                wb_scales[0, 4 * q : 4 * q + 4, :].bitcast(I32),
            )
        resid = sb.tile([P, CHUNKS, N], F32, name="resid")
        nc.sync.dma_start(resid[:], rs.rearrange("(c p) n -> p c n", p=P))

        w_code = sb.tile([P, PASSES, PACK, P], U16, name="w_code", align_bytes=64)
        nc.vector.tensor_copy(w_code[:], w_raw[:].rearrange("p a (q t) -> p a t q", t=PACK))
        w_scale = sb.tile([P, PASSES, PACK, P], U8, name="w_scale", align_bytes=64)
        nc.vector.tensor_copy(w_scale[:], w_scale_raw[:].rearrange("p a (q t) -> p a t q", t=PACK))

        picked = [sb.tile([P, J], F32, name=f"picked{i}") for i in range(PASSES * PACK)]
        pairs = [sb.tile([P, 2, J, 2], BF16, name=f"pairs{a}") for a in range(PASSES)]
        u = [sb.tile([P, J, PACK], BF16, name=f"u{a}", align_bytes=64) for a in range(PASSES)]
        u_code = [sb.tile([P, J], U32, name=f"u_code{a}", align_bytes=64) for a in range(PASSES)]
        u_scale = [sb.tile([P, J], U8, name=f"u_scale{a}", align_bytes=64) for a in range(PASSES)]
        first = [ps.tile([P, PACK, CHUNK], F32, name=f"first{c}") for c in range(CHUNKS)]

        def pick(i, lo, hi):
            nc.scalar.activation(picked[i][:, lo:hi], x_plane[i][:].indirect(x_list[:, lo // 16 : hi // 16]), ACT.Copy)

        def scale(i, lo, hi):
            a, t = divmod(i, PACK)
            nc.vector.tensor_scalar(
                scaled[i // 2][:, i % 2, PAD + lo : PAD + hi], picked[i][:, lo:hi], factor[:, a, t : t + 1], None, ALU.mult
            )

        def steps(h, lo, hi):
            nc.vector.scalar_tensor_tensor(
                pairs[h // 2][:, h % 2, lo:hi, :],
                scaled[h][:, :, PAD - 1 + lo : PAD - 1 + hi].rearrange("p e j -> p j e"),
                -0.6,
                scaled[h][:, :, PAD + lo : PAD + hi].rearrange("p e j -> p j e"),
                ALU.mult,
                ALU.add,
            )

        def weave(a, lo, hi):
            words = pairs[a][:].rearrange("p h j e -> p h (j e)").bitcast(I32)
            nc.vector.tensor_copy(u[a][:, lo:hi, :].bitcast(I32), words[:, :, lo:hi].rearrange("p h j -> p j h"))

        def quantise_u(a, lo, hi):
            nc.vector.quantize_mx(
                out=u_code[a][:, lo:hi].bitcast(E4M3),
                scales=u_scale[a][:, lo:hi],
                in_=u[a][:, lo:hi, :].rearrange("p j t -> p (j t)"),
            )

        def first_product(a, c):
            for t in range(PACK):
                nc.tensor.matmul_mx(
                    out=first[c][:, t, :],
                    lhsT=w_code[:, a, t, :].bitcast(E2M1),
                    lhsT_scale=w_scale[:, a, t, :],
                    rhs=u_code[a][:, cols(c)].bitcast(E4M3),
                    rhs_scale=u_scale[a][:, cols(c)],
                    start=(a == 0 and t == 0),
                    stop=(a == PASSES - 1 and t == PACK - 1),
                )

        last = PASSES * PACK - 1
        for i in range(last):
            pick(i, 0, J)
            scale(i, 0, J)
            if i % 2 == 1:
                steps(i // 2, 0, J)
            if i == PACK - 1:
                weave(0, 0, J)
                quantise_u(0, 0, J)
                for c in range(CHUNKS):
                    first_product(0, c)
        for c in range(CHUNKS):
            lo, hi = c * CHUNK, (c + 1) * CHUNK
            pick(last, lo, hi)
            scale(last, lo, hi)
            steps(last // 2, lo, hi)
            weave(1, lo, hi)
            quantise_u(1, lo, hi)
            first_product(1, c)

        tb_picked = [sb.tile([P, PACK, CHUNK], F32, name=f"tb_picked{c}") for c in range(CHUNKS)]
        for c in range(CHUNKS):
            for t in range(PACK):
                nc.scalar.activation(tb_picked[c][:, t, :], tb_plane[t].indirect(tb_list[:, entries(c)]), ACT.Copy)

        resid_part = sb.tile([P, CHUNKS, N], F32, name="resid_part")
        for c in range(CHUNKS):
            hid = sb.tile([P, CHUNK, PACK], BF16, name=f"hid{c}", align_bytes=64)
            nc.vector.scalar_tensor_tensor(
                hid[:],
                first[c][:].rearrange("p t j -> p j t"),
                0.0,
                tb_picked[c][:].rearrange("p t j -> p j t"),
                ALU.max,
                ALU.mult,
            )
            hid_code = sb.tile([P, CHUNK], U32, name=f"hid_code{c}", align_bytes=64)
            hid_scale = sb.tile([P, CHUNK], U8, name=f"hid_scale{c}", align_bytes=64)
            nc.vector.quantize_mx(
                out=hid_code[:].bitcast(E4M3), scales=hid_scale[:], in_=hid[:].rearrange("p j t -> p (j t)")
            )
            second = ps.tile([P, N], F32, name=f"second{c}")
            nc.tensor.matmul_mx(
                out=second[:],
                lhsT=hid_code[:].bitcast(E4M3),
                lhsT_scale=hid_scale[:],
                rhs=wb_code[:].bitcast(E5M2),
                rhs_scale=wb_scale[:],
                start=True,
                stop=True,
            )
            nc.scalar.activation(resid_part[:, c, :], resid[:, c, :], ACT.Copy, scale=0.3)
            size = sb.tile([P, N], F32, name=f"size{c}")
            nc.scalar.activation(size[:], second[:], ACT.Abs)
            divisor = sb.tile([P, 1], F32, name=f"divisor{c}")
            nc.vector.tensor_scalar(size[:], size[:], 0.2, None, ALU.add, ALU.max, accum_out=divisor[:])
            inverse = sb.tile([P, 1], F32, name=f"inverse{c}")
            nc.vector.reciprocal(inverse[:], divisor[:])
            result = sb.tile([P, N], F32, name=f"result{c}")
            nc.vector.scalar_tensor_tensor(result[:], second[:], inverse[:], resid_part[:, c, :], ALU.mult, ALU.add)
            nc.sync.dma_start(out[cols(c), :], result[:])
